import numpy as np
import ml_dtypes


def mxq(x, axis, fmt="e4m3"):
    dtype, down = {"e4m3": (ml_dtypes.float8_e4m3fn, 7), "e5m2": (ml_dtypes.float8_e5m2, 14)}[fmt]
    v = np.moveaxis(np.asarray(x, np.float32).astype(ml_dtypes.bfloat16).astype(np.float64), axis, -1)
    blocks = v.reshape(v.shape[:-1] + (-1, 32))
    amax = np.abs(blocks).max(-1, keepdims=True)
    byte = np.maximum(np.where(amax > 0, np.frexp(amax)[1] - 1 + 127, 0) - down, 1)
    scale = np.exp2(byte - 127.0)
    codes = (blocks / scale).astype(np.float32).astype(dtype).astype(np.float64)
    return np.moveaxis((codes * scale).reshape(v.shape), -1, axis)


WIDE = False


def mx_kscale(k):
    if not WIDE:
        return np.ones(k)
    levels = np.array([10, -10, 5, -5, 0])
    if k % 512:
        return np.exp2(np.random.permutation(np.resize(levels, k // 32))).repeat(32)
    a = np.empty((k // 512, 16))
    for p in range(k // 512):
        a[p, :8] = np.random.permutation(np.resize(levels, 8))
        for g in range(8):
            far = levels[np.abs(levels - a[p, g]) >= 10]
            a[p, g + 8] = far[np.random.randint(len(far))]
    return np.exp2(a.ravel()).repeat(32)


def f64(x):
    return np.asarray(x).astype(np.float64)


def striped(idx):
    return np.tile(idx.reshape(-1, 16).T, (8, 1)).astype(np.uint16)


def unstriped(offs):
    return offs[:16].T.reshape(-1).astype(np.int64)


E2M1 = np.array([0.0, 0.5, 1.0, 1.5, 2.0, 3.0, 4.0, 6.0, -0.0, -0.5, -1.0, -1.5, -2.0, -3.0, -4.0, -6.0])


def pack_weight(w, fmt):
    k, n = w.shape
    w = f64(np.asarray(w, np.float32).astype(ml_dtypes.bfloat16)).reshape(k // 32, 32, n)
    amax = np.abs(w).max(1)
    if fmt == "e4m3":
        byte = np.frexp(amax)[1] - 1 + 127 - 7
    else:
        mant, ex = np.frexp(amax / 6.0)
        byte = np.where(mant > 0.5, ex, ex - 1) + 127
    byte = np.clip(np.where(amax > 0, byte, 1), 1, 254)
    scaled = (w * np.exp2(127.0 - byte)[:, None, :]).reshape(k, n).astype(np.float32)
    by_word = np.ascontiguousarray(scaled.reshape(k // 512, 128, 4, n).transpose(0, 1, 3, 2))
    if fmt == "e4m3":
        words = by_word.astype(ml_dtypes.float8_e4m3fn).view(np.uint8)
    else:
        c = by_word.astype(ml_dtypes.float4_e2m1fn).view(np.uint8) & 0xF
        words = (c[..., 0::2] | (c[..., 1::2] << 4)).reshape(k // 512, 128, 2 * n)
    return np.ascontiguousarray(words), np.ascontiguousarray(byte.astype(np.uint8).reshape(k // 512, 16, n))


def unpack_weight(words, scales, fmt):
    g, _, n = scales.shape
    words = np.ascontiguousarray(words).reshape(g, 128, n, -1)
    if fmt == "e4m3":
        vals = words.view(ml_dtypes.float8_e4m3fn).astype(np.float64)
    else:
        nib = np.empty((g, 128, n, 4), np.uint8)
        nib[..., 0::2] = words & 0xF
        nib[..., 1::2] = words >> 4
        vals = E2M1[nib]
    vals = vals * np.repeat(np.exp2(scales.astype(np.float64) - 127.0), 8, axis=1)[..., None]
    return vals.transpose(0, 1, 3, 2).reshape(g * 512, n)


def silu(v):
    return v / (1.0 + np.exp(-np.maximum(v, -700.0)))


K, T, E, C, N = 1536, 640, 8, 128, 384
TOP = 3
PAD = 64


def by_expert(wq, xq):
    return np.concatenate([wq[e].T @ xq[:, e * C:(e + 1) * C] for e in range(E)], axis=1)


def setup_inputs():
    n = np.random.standard_normal
    s = mx_kscale(K)[:, None]
    slot_token = np.empty(E * C, np.int64); pos = np.tile(E * C + np.arange(T) % PAD, (TOP, 1)); taken = np.zeros(T, np.int64)
    liked = np.random.randn(T)
    for e in np.random.permutation(E):
        free = np.flatnonzero(taken < TOP); pick = np.random.permutation(free[np.argsort(-(liked[free] + np.random.gumbel(size=free.size)))[:C]]); slot_token[e * C:(e + 1) * C] = pick
        pos[taken[pick], pick] = e * C + np.arange(C); taken[pick] += 1
    g = np.random.uniform(0.2, 0.8, (TOP, T))
    w = [pack_weight(m, "e2m1") for m in n((E, K, N)) / np.sqrt(K) / s[None]]
    return {
        "xT": (n((K, T)) * s).astype(np.float32),
        "w_words": np.stack([m[0] for m in w]),
        "w_scales": np.stack([m[1] for m in w]),
        "b": (0.3 * n((N, E))).astype(np.float32),
        "gate": np.stack([np.tile(r, (N, 1)) for r in g]).astype(np.float32),
        "offs": striped(slot_token),
        "pos1": striped(pos[0]),
        "pos2": striped(pos[1]),
        "pos3": striped(pos[2]),
    }


def reference(xT, w_words, w_scales, b, gate, offs, pos1, pos2, pos3):
    idx = unstriped(offs)
    w = np.stack([unpack_weight(w_words[e], w_scales[e], "e2m1") for e in range(E)])
    xq = mxq(f64(xT)[:, idx], 0, "e4m3")
    y = by_expert(w, xq)
    y = silu(y + np.repeat(f64(b), C, axis=1))
    y = np.concatenate([y, np.zeros((N, PAD))], axis=1)
    return sum(f64(gate[r]) * y[:, unstriped(p)] for r, p in enumerate((pos1, pos2, pos3)))

@@ -1,0 +1,248 @@
+from contextlib import ExitStack
+
+import concourse.mybir as mybir
+from concourse.masks import make_identity
+
+K, T, E, C, N = 1536, 640, 8, 128, 384
+TOP = 3
+PAD = 64
+SLOTS = E * C
+
+FLOPS = 2 * K * N * SLOTS
+
+F32 = mybir.dt.float32
+BF16 = mybir.dt.bfloat16
+I32 = mybir.dt.int32
+U32 = mybir.dt.uint32
+U16 = mybir.dt.uint16
+U8 = mybir.dt.uint8
+FP8X4 = mybir.dt.float8_e4m3fn_x4
+FP4X4 = mybir.dt.float4_e2m1fn_x4
+ACT = mybir.ActivationFunctionType
+ALU = mybir.AluOpType
+
+P = 128
+PACK = 4
+K_PASS = P * PACK
+PASSES = K // K_PASS
+CHUNKS = N // P
+TOKEN_PIECES = ((0, 256), (256, 512), (512, 640))
+SLOT_PIECES = ((0, 384), (384, 768), (768, 1024))
+DEFERRED = ((1, 1), (1, 2))
+BANK = 512
+SHIFT_ROWS = ((0, 64), (64, 96), (96, 100))
+
+
+def tile_moe_ecr_lin_silu_kernel(tc, xT, w_words, w_scales, b, gate, offs, pos1, pos2, pos3, out):
+    nc = tc.nc
+    with ExitStack() as ctx:
+        keep = ctx.enter_context(tc.tile_pool(name="keep", bufs=1))
+        psum = ctx.enter_context(tc.psum_pool(name="psum", bufs=8))
+
+        slot_list = keep.tile([P, SLOTS // 16], U16, name="slot_list")
+        pos_lists = [keep.tile([P, T // 16], U16, name=f"pos_list{r}") for r in range(TOP)]
+        bias = keep.tile([P, CHUNKS, E], F32, name="bias")
+        tok_codes = [keep.tile([P, T], U32, name=f"tok_codes{a}", align_bytes=64) for a in range(PASSES)]
+        slot_codes = {
+            (a, s): keep.tile([P, s1 - s0], U32, name=f"slot_codes{a}_{s0}", align_bytes=64)
+            for a in range(PASSES)
+            for s, (s0, s1) in enumerate(SLOT_PIECES)
+            if (a, s) not in DEFERRED
+        }
+        slot_scales = [keep.tile([P, SLOTS], U8, name=f"slot_scales{a}", align_bytes=64) for a in range(PASSES)]
+        w_codes0 = keep.tile([P, E * PASSES, 2 * P], U8, name="w_codes0", align_bytes=64)
+        w_plane0 = keep.tile([P, E * PASSES, P], U8, name="w_plane0", align_bytes=64)
+        w_plane12 = keep.tile([P, E * PASSES, 2 * P], U8, name="w_plane12", align_bytes=64)
+        identity = keep.tile([P, P], F32, name="identity")
+        first_gate = keep.tile([P, 1, T], F32, name="first_gate")
+        ys = [keep.tile([P, SLOTS + PAD], F32, name=f"y{c}") for c in range(CHUNKS)]
+        zeros = keep.tile([P, PAD], F32, name="zeros")
+        prods = [keep.tile([P, TOP, T], F32, name=f"prods{c}") for c in range(CHUNKS)]
+        results = [keep.tile([P, T], F32, name=f"result{c}") for c in range(CHUNKS)]
+
+        with tc.tile_pool(name="stage", bufs=1) as stage:
+            raw = [[stage.tile([P, PACK, t1 - t0], F32, name=f"raw{a}_{t0}") for t0, t1 in TOKEN_PIECES] for a in range(PASSES)]
+            grouped = [[stage.tile([P, t1 - t0, PACK], BF16, name=f"grouped{a}_{t0}", align_bytes=64) for t0, t1 in TOKEN_PIECES] for a in range(PASSES)]
+            tok_scales = stage.tile([P, T], U8, name="tok_scales", align_bytes=64)
+
+            nc.vector.memset(zeros[:], 0.0)
+            nc.scalar.activation(out=ys[0][:, SLOTS:], in_=zeros[:], func=ACT.Silu)
+            nc.gpsimd.memset(tok_scales[:], 0)
+            make_identity(nc, identity[:])
+            for plane in (w_plane0, w_plane12):
+                nc.vector.memset(plane[:].rearrange("p g n -> p (g n)").bitcast(I32), 0)
+            for a in range(1, PASSES):
+                nc.vector.memset(slot_scales[a][:].bitcast(I32), 0)
+            for c in range(1, CHUNKS):
+                nc.vector.memset(ys[c][:, SLOTS:], 0.0)
+
+            def load_x(a):
+                rows = xT[a * K_PASS : (a + 1) * K_PASS, :].rearrange("(p j) t -> p j t", j=PACK)
+                for i, (t0, t1) in enumerate(TOKEN_PIECES):
+                    nc.sync.dma_start(out=raw[a][i][:], in_=rows[:, :, t0:t1])
+
+            def load_planes(plane, n0, n1):
+                rows = w_scales.rearrange("e a q n -> q (e a) n")
+                for quad in range(4):
+                    nc.sync.dma_start(
+                        out=plane[32 * quad : 32 * quad + 4, :, :].bitcast(I32),
+                        in_=rows[4 * quad : 4 * quad + 4, :, n0:n1].bitcast(I32),
+                    )
+
+            def load_w(codes, g0, g1, n0, n1):
+                words = w_words.rearrange("e a p b -> p (e a) b")
+                nc.sync.dma_start(out=codes[:].bitcast(I32), in_=words[:, g0:g1, 2 * n0 : 2 * n1].bitcast(I32))
+
+            def load_gate(dst, c, r0, r1):
+                nc.sync.dma_start(out=dst[:], in_=gate[r0:r1, c * P : (c + 1) * P, :].rearrange("r p t -> p r t"))
+
+            load_x(0)
+            nc.sync.dma_start(slot_list[:], offs)
+            load_x(1)
+            load_x(2)
+            load_w(w_codes0, 0, E * PASSES, 0, P)
+            load_planes(w_plane0, 0, P)
+            nc.sync.dma_start(out=bias[:], in_=b.rearrange("(c p) e -> p c e", p=P))
+            for r, pos in enumerate((pos1, pos2, pos3)):
+                nc.sync.dma_start(pos_lists[r][:], pos)
+            load_gate(first_gate, 0, 0, 1)
+            load_planes(w_plane12, P, N)
+
+            def interleave(a, i, on_vector):
+                src = raw[a][i][:].rearrange("p j (c i) -> p c j i", i=4)
+                dst = grouped[a][i][:].rearrange("p (c i) j -> p c j i", i=4)
+                if on_vector:
+                    nc.vector.tensor_copy(out=dst, in_=src)
+                else:
+                    nc.scalar.activation(out=dst, in_=src, func=ACT.Copy)
+
+            def quantize(a, i):
+                t0, t1 = TOKEN_PIECES[i]
+                nc.vector.quantize_mx(
+                    out=tok_codes[a][:, t0:t1].bitcast(FP8X4),
+                    scales=tok_scales[4 * a :, t0:t1],
+                    in_=grouped[a][i][:].rearrange("p t j -> p (t j)"),
+                )
+
+            def gather_words(a, s):
+                s0, s1 = SLOT_PIECES[s]
+                nc.vector.tensor_copy(slot_codes[a, s][:], tok_codes[a][:].indirect(slot_list[:, s0 // 16 : s1 // 16]))
+
+            def gather_bytes(s):
+                s0, s1 = SLOT_PIECES[s]
+                nc.vector.tensor_copy(slot_scales[0][:, s0:s1], tok_scales[:].indirect(slot_list[:, s0 // 16 : s1 // 16]))
+
+            def shift(s0, s1):
+                for a in range(1, PASSES):
+                    for r0, r1 in SHIFT_ROWS:
+                        nc.scalar.dma_start(
+                            out=slot_scales[a][r0:r1, s0:s1].bitcast(I32),
+                            in_=slot_scales[0][r0 + 4 * a : r1 + 4 * a, s0:s1].bitcast(I32),
+                        )
+
+            for a in range(PASSES):
+                for i in range(len(TOKEN_PIECES)):
+                    interleave(a, i, (a, i) in ((0, 1), (2, 2)))
+                for i in range(len(TOKEN_PIECES)):
+                    quantize(a, i)
+                if a < PASSES - 1:
+                    for s in range(len(SLOT_PIECES)):
+                        if (a, s) not in DEFERRED:
+                            gather_words(a, s)
+            for s in range(len(SLOT_PIECES)):
+                gather_bytes(s)
+            shift(0, SLOTS)
+
+        late = ctx.enter_context(tc.tile_pool(name="late", bufs=1))
+        for a, s in DEFERRED:
+            s0, s1 = SLOT_PIECES[s]
+            slot_codes[a, s] = late.tile([P, s1 - s0], U32, name=f"slot_codes{a}_{s0}", align_bytes=64)
+        for s in range(len(SLOT_PIECES)):
+            if (1, s) in DEFERRED:
+                gather_words(1, s)
+            gather_words(PASSES - 1, s)
+
+        gates = {(c, r): late.tile([P, 1, T], F32, name=f"gate{c}_{r}") for c, r in ((0, 1), (0, 2))}
+        gates[0, 0] = first_gate
+        half = E * PASSES // 2
+        w_codes12 = [late.tile([P, half, 4 * P], U8, name=f"w_codes12_{h}", align_bytes=64) for h in range(2)]
+        later_gates = [late.tile([P, TOP, T], F32, name=f"gates{c}") for c in range(1, CHUNKS)]
+        load_gate(gates[0, 1], 0, 1, 2)
+        load_w(w_codes12[0], 0, half, P, N)
+        load_gate(gates[0, 2], 0, 2, 3)
+        load_w(w_codes12[1], half, 2 * half, P, N)
+        load_gate(later_gates[0], 1, 0, TOP)
+        load_gate(later_gates[1], 2, 0, TOP)
+
+        def gate_rows(c, r):
+            return gates[c, r][:, 0, :] if c == 0 else later_gates[c - 1][:, r, :]
+
+        def experts(c):
+            for e in range(E):
+                acc = psum.tile([P, C], F32, name="acc", tag="bank")
+                cols = slice(e * C, (e + 1) * C)
+                s = [s0 <= e * C < s1 for s0, s1 in SLOT_PIECES].index(True)
+                in_piece = slice(e * C - SLOT_PIECES[s][0], (e + 1) * C - SLOT_PIECES[s][0])
+                for a in range(PASSES):
+                    g = e * PASSES + a
+                    w_code = w_codes0[:, g, :] if c == 0 else w_codes12[g // half][:, g % half, (c - 1) * 2 * P : c * 2 * P]
+                    nc.tensor.matmul_mx(
+                        out=acc[:],
+                        lhsT=w_code.bitcast(FP4X4),
+                        lhsT_scale=w_plane0[:, g, :] if c == 0 else w_plane12[:, g, (c - 1) * P : c * P],
+                        rhs=slot_codes[a, s][:, in_piece].bitcast(FP8X4),
+                        rhs_scale=slot_scales[a][:, cols],
+                        start=(a == 0),
+                        stop=(a == PASSES - 1),
+                    )
+                nc.scalar.activation(out=ys[c][:, cols], in_=acc[:], func=ACT.Silu, bias=bias[:, c, e : e + 1])
+
+        for c in range(CHUNKS):
+            experts(c)
+
+        def product(c, t0, t1, r):
+            nc.vector.tensor_tensor(
+                prods[c][:, r, t0:t1], ys[c][:].indirect(pos_lists[r][:, t0 // 16 : t1 // 16]), gate_rows(c, r)[:, t0:t1], ALU.mult
+            )
+
+        def store(c, t0, t1):
+            nc.sync.dma_start(out=out[c * P : (c + 1) * P, t0:t1], in_=results[c][:, t0:t1])
+
+        def sum_on_tensor(c):
+            turned = late.tile([P, T], F32, name=f"turned{c}")
+            for t0, t1 in ((0, BANK), (BANK, T)):
+                sums = psum.tile([P, t1 - t0], F32, name="sums", tag="bank")
+                for t in range(t0, t1, P):
+                    for r in range(TOP):
+                        nc.tensor.matmul(
+                            sums[:, t - t0 : t - t0 + P], prods[c][:, r, t : t + P], identity[:], start=(r == 0), stop=(r == TOP - 1), is_transpose=True
+                        )
+                nc.scalar.copy(out=turned[:, t0:t1], in_=sums[:])
+            for t0, t1 in ((0, BANK), (BANK, T)):
+                back = psum.tile([P, t1 - t0], F32, name="back", tag="bank")
+                for t in range(t0, t1, P):
+                    nc.tensor.transpose(back[:, t - t0 : t - t0 + P], turned[:, t : t + P], identity[:])
+                nc.scalar.copy(out=results[c][:, t0:t1], in_=back[:])
+            store(c, 0, T)
+
+        def first_sum(c, t0, t1):
+            nc.vector.tensor_tensor(results[c][:, t0:t1], prods[c][:, 0, t0:t1], prods[c][:, 1, t0:t1], ALU.add)
+
+        def last_sum(c, t0, t1):
+            nc.vector.tensor_tensor(results[c][:, t0:t1], results[c][:, t0:t1], prods[c][:, 2, t0:t1], ALU.add)
+            store(c, t0, t1)
+
+        for c in range(CHUNKS - 1):
+            for r in range(TOP):
+                product(c, 0, T, r)
+            sum_on_tensor(c)
+        left, right = (CHUNKS - 1, 0, T // 2), (CHUNKS - 1, T // 2, T)
+        for r in range(TOP):
+            product(*left, r)
+        first_sum(*left)
+        product(*right, 0)
+        last_sum(*left)
+        product(*right, 1)
+        product(*right, 2)
+        first_sum(*right)
+        last_sum(*right)

@@ -26,10 +26,16 @@ PACK = 4
 K_PASS = P * PACK
 PASSES = K // K_PASS
 CHUNKS = N // P
-TOKEN_PIECES = ((0, 256), (256, 512), (512, 640))
+QUANT_PIECES = ((0, 256), (256, 512), (512, 640))
+SHARED_COPY = ((0, 256, True), (256, 320, True), (320, 512, False), (512, 640, False))
+SCALAR_COPY = ((0, 256, False), (256, 512, False), (512, 640, False))
+COPY_PIECES = (SHARED_COPY, SCALAR_COPY, SHARED_COPY)
 SLOT_PIECES = ((0, 384), (384, 768), (768, 1024))
-DEFERRED = ((1, 1), (1, 2))
+DEFERRED = ((1, 0), (1, 1), (1, 2))
+W_GROUP = 2 * PASSES
+EARLY_W_GROUPS = 2
 BANK = 512
+LAST_SPANS = ((0, 384), (384, 640))
 SHIFT_ROWS = ((0, 64), (64, 96), (96, 100))
 
 
@@ -50,36 +56,36 @@ def tile_moe_ecr_lin_silu_kernel(tc, xT, w_words, w_scales, b, gate, offs, pos1,
             if (a, s) not in DEFERRED
         }
         slot_scales = [keep.tile([P, SLOTS], U8, name=f"slot_scales{a}", align_bytes=64) for a in range(PASSES)]
-        w_codes0 = keep.tile([P, E * PASSES, 2 * P], U8, name="w_codes0", align_bytes=64)
-        w_plane0 = keep.tile([P, E * PASSES, P], U8, name="w_plane0", align_bytes=64)
-        w_plane12 = keep.tile([P, E * PASSES, 2 * P], U8, name="w_plane12", align_bytes=64)
+        w_codes01 = [keep.tile([P, W_GROUP, 4 * P], U8, name=f"w_codes01_{h}", align_bytes=64) for h in range(EARLY_W_GROUPS)]
+        w_plane01 = keep.tile([P, E * PASSES, 2 * P], U8, name="w_plane01", align_bytes=64)
         identity = keep.tile([P, P], F32, name="identity")
-        first_gate = keep.tile([P, 1, T], F32, name="first_gate")
         ys = [keep.tile([P, SLOTS + PAD], F32, name=f"y{c}") for c in range(CHUNKS)]
         zeros = keep.tile([P, PAD], F32, name="zeros")
         prods = [keep.tile([P, TOP, T], F32, name=f"prods{c}") for c in range(CHUNKS)]
         results = [keep.tile([P, T], F32, name=f"result{c}") for c in range(CHUNKS)]
 
         with tc.tile_pool(name="stage", bufs=1) as stage:
-            raw = [[stage.tile([P, PACK, t1 - t0], F32, name=f"raw{a}_{t0}") for t0, t1 in TOKEN_PIECES] for a in range(PASSES)]
-            grouped = [[stage.tile([P, t1 - t0, PACK], BF16, name=f"grouped{a}_{t0}", align_bytes=64) for t0, t1 in TOKEN_PIECES] for a in range(PASSES)]
+            raw = [stage.tile([P, PACK, T], F32, name=f"raw{a}") for a in range(PASSES)]
+            grouped = [stage.tile([P, T, PACK], BF16, name=f"grouped{a}", align_bytes=64) for a in range(PASSES)]
             tok_scales = stage.tile([P, T], U8, name="tok_scales", align_bytes=64)
 
             nc.vector.memset(zeros[:], 0.0)
             nc.scalar.activation(out=ys[0][:, SLOTS:], in_=zeros[:], func=ACT.Silu)
-            nc.gpsimd.memset(tok_scales[:], 0)
-            make_identity(nc, identity[:])
-            for plane in (w_plane0, w_plane12):
-                nc.vector.memset(plane[:].rearrange("p g n -> p (g n)").bitcast(I32), 0)
+            nc.vector.memset(tok_scales[:].bitcast(I32), 0)
+            nc.vector.memset(w_plane01[:].rearrange("p g n -> p (g n)").bitcast(I32), 0)
             for a in range(1, PASSES):
                 nc.vector.memset(slot_scales[a][:].bitcast(I32), 0)
             for c in range(1, CHUNKS):
                 nc.vector.memset(ys[c][:, SLOTS:], 0.0)
+            make_identity(nc, identity[:])
 
             def load_x(a):
                 rows = xT[a * K_PASS : (a + 1) * K_PASS, :].rearrange("(p j) t -> p j t", j=PACK)
-                for i, (t0, t1) in enumerate(TOKEN_PIECES):
-                    nc.sync.dma_start(out=raw[a][i][:], in_=rows[:, :, t0:t1])
+                nc.sync.dma_start(out=raw[a][:], in_=rows)
+
+            def load_w(codes, g0, g1, n0, n1):
+                words = w_words.rearrange("e a p b -> p (e a) b")
+                nc.sync.dma_start(out=codes[:].bitcast(I32), in_=words[:, g0:g1, 2 * n0 : 2 * n1].bitcast(I32))
 
             def load_planes(plane, n0, n1):
                 rows = w_scales.rearrange("e a q n -> q (e a) n")
@@ -89,39 +95,33 @@ def tile_moe_ecr_lin_silu_kernel(tc, xT, w_words, w_scales, b, gate, offs, pos1,
                         in_=rows[4 * quad : 4 * quad + 4, :, n0:n1].bitcast(I32),
                     )
 
-            def load_w(codes, g0, g1, n0, n1):
-                words = w_words.rearrange("e a p b -> p (e a) b")
-                nc.sync.dma_start(out=codes[:].bitcast(I32), in_=words[:, g0:g1, 2 * n0 : 2 * n1].bitcast(I32))
-
-            def load_gate(dst, c, r0, r1):
-                nc.sync.dma_start(out=dst[:], in_=gate[r0:r1, c * P : (c + 1) * P, :].rearrange("r p t -> p r t"))
+            def load_gates(c, r0, r1):
+                nc.sync.dma_start(out=gates[c][:, r0:r1, :], in_=gate[r0:r1, c * P : (c + 1) * P, :].rearrange("r p t -> p r t"))
 
             load_x(0)
             nc.sync.dma_start(slot_list[:], offs)
             load_x(1)
             load_x(2)
-            load_w(w_codes0, 0, E * PASSES, 0, P)
-            load_planes(w_plane0, 0, P)
             nc.sync.dma_start(out=bias[:], in_=b.rearrange("(c p) e -> p c e", p=P))
             for r, pos in enumerate((pos1, pos2, pos3)):
                 nc.sync.dma_start(pos_lists[r][:], pos)
-            load_gate(first_gate, 0, 0, 1)
-            load_planes(w_plane12, P, N)
+            load_planes(w_plane01, 0, 2 * P)
+            for h in range(EARLY_W_GROUPS):
+                load_w(w_codes01[h], h * W_GROUP, (h + 1) * W_GROUP, 0, 2 * P)
 
-            def interleave(a, i, on_vector):
-                src = raw[a][i][:].rearrange("p j (c i) -> p c j i", i=4)
-                dst = grouped[a][i][:].rearrange("p (c i) j -> p c j i", i=4)
+            def interleave(a, t0, t1, on_vector):
+                src = raw[a][:, :, t0:t1].rearrange("p j (c i) -> p c j i", i=4)
+                dst = grouped[a][:, t0:t1, :].rearrange("p (c i) j -> p c j i", i=4)
                 if on_vector:
                     nc.vector.tensor_copy(out=dst, in_=src)
                 else:
                     nc.scalar.activation(out=dst, in_=src, func=ACT.Copy)
 
-            def quantize(a, i):
-                t0, t1 = TOKEN_PIECES[i]
+            def quantize(a, t0, t1):
                 nc.vector.quantize_mx(
                     out=tok_codes[a][:, t0:t1].bitcast(FP8X4),
                     scales=tok_scales[4 * a :, t0:t1],
-                    in_=grouped[a][i][:].rearrange("p t j -> p (t j)"),
+                    in_=grouped[a][:, t0:t1, :].rearrange("p t j -> p (t j)"),
                 )
 
             def gather_words(a, s):
@@ -135,16 +135,16 @@ def tile_moe_ecr_lin_silu_kernel(tc, xT, w_words, w_scales, b, gate, offs, pos1,
             def shift(s0, s1):
                 for a in range(1, PASSES):
                     for r0, r1 in SHIFT_ROWS:
-                        nc.scalar.dma_start(
+                        nc.sync.dma_start(
                             out=slot_scales[a][r0:r1, s0:s1].bitcast(I32),
                             in_=slot_scales[0][r0 + 4 * a : r1 + 4 * a, s0:s1].bitcast(I32),
                         )
 
             for a in range(PASSES):
-                for i in range(len(TOKEN_PIECES)):
-                    interleave(a, i, (a, i) in ((0, 1), (2, 2)))
-                for i in range(len(TOKEN_PIECES)):
-                    quantize(a, i)
+                for piece in COPY_PIECES[a]:
+                    interleave(a, *piece)
+                for piece in QUANT_PIECES:
+                    quantize(a, *piece)
                 if a < PASSES - 1:
                     for s in range(len(SLOT_PIECES)):
                         if (a, s) not in DEFERRED:
@@ -158,24 +158,28 @@ def tile_moe_ecr_lin_silu_kernel(tc, xT, w_words, w_scales, b, gate, offs, pos1,
             s0, s1 = SLOT_PIECES[s]
             slot_codes[a, s] = late.tile([P, s1 - s0], U32, name=f"slot_codes{a}_{s0}", align_bytes=64)
         for s in range(len(SLOT_PIECES)):
+            gather_words(PASSES - 1, s)
             if (1, s) in DEFERRED:
                 gather_words(1, s)
-            gather_words(PASSES - 1, s)
 
-        gates = {(c, r): late.tile([P, 1, T], F32, name=f"gate{c}_{r}") for c, r in ((0, 1), (0, 2))}
-        gates[0, 0] = first_gate
         half = E * PASSES // 2
-        w_codes12 = [late.tile([P, half, 4 * P], U8, name=f"w_codes12_{h}", align_bytes=64) for h in range(2)]
-        later_gates = [late.tile([P, TOP, T], F32, name=f"gates{c}") for c in range(1, CHUNKS)]
-        load_gate(gates[0, 1], 0, 1, 2)
-        load_w(w_codes12[0], 0, half, P, N)
-        load_gate(gates[0, 2], 0, 2, 3)
-        load_w(w_codes12[1], half, 2 * half, P, N)
-        load_gate(later_gates[0], 1, 0, TOP)
-        load_gate(later_gates[1], 2, 0, TOP)
-
-        def gate_rows(c, r):
-            return gates[c, r][:, 0, :] if c == 0 else later_gates[c - 1][:, r, :]
+        for h in range(EARLY_W_GROUPS, E * PASSES // W_GROUP):
+            w_codes01.append(late.tile([P, W_GROUP, 4 * P], U8, name=f"w_codes01_{h}", align_bytes=64))
+            load_w(w_codes01[h], h * W_GROUP, (h + 1) * W_GROUP, 0, 2 * P)
+        w_codes2 = [late.tile([P, half, 2 * P], U8, name=f"w_codes2_{h}", align_bytes=64) for h in range(2)]
+        w_plane2 = late.tile([P, E * PASSES, P], U8, name="w_plane2", align_bytes=64)
+        gates = [late.tile([P, TOP, T], F32, name=f"gates{c}") for c in range(CHUNKS)]
+        nc.gpsimd.memset(w_plane2[:].rearrange("p g n -> p (g n)").bitcast(I32), 0)
+        load_gates(0, 0, 1)
+        load_gates(0, 1, TOP)
+        load_planes(w_plane2, 2 * P, N)
+        load_gates(1, 0, 1)
+        load_w(w_codes2[0], 0, half, 2 * P, N)
+        load_gates(1, 1, 2)
+        load_w(w_codes2[1], half, 2 * half, 2 * P, N)
+        load_gates(1, 2, 3)
+        load_gates(2, 0, 1)
+        load_gates(2, 1, TOP)
 
         def experts(c):
             for e in range(E):
@@ -185,11 +189,11 @@ def tile_moe_ecr_lin_silu_kernel(tc, xT, w_words, w_scales, b, gate, offs, pos1,
                 in_piece = slice(e * C - SLOT_PIECES[s][0], (e + 1) * C - SLOT_PIECES[s][0])
                 for a in range(PASSES):
                     g = e * PASSES + a
-                    w_code = w_codes0[:, g, :] if c == 0 else w_codes12[g // half][:, g % half, (c - 1) * 2 * P : c * 2 * P]
+                    w_code = w_codes01[g // W_GROUP][:, g % W_GROUP, c * 2 * P : (c + 1) * 2 * P] if c < 2 else w_codes2[g // half][:, g % half, :]
                     nc.tensor.matmul_mx(
                         out=acc[:],
                         lhsT=w_code.bitcast(FP4X4),
-                        lhsT_scale=w_plane0[:, g, :] if c == 0 else w_plane12[:, g, (c - 1) * P : c * P],
+                        lhsT_scale=w_plane01[:, g, c * P : (c + 1) * P] if c < 2 else w_plane2[:, g, :],
                         rhs=slot_codes[a, s][:, in_piece].bitcast(FP8X4),
                         rhs_scale=slot_scales[a][:, cols],
                         start=(a == 0),
@@ -200,17 +204,16 @@ def tile_moe_ecr_lin_silu_kernel(tc, xT, w_words, w_scales, b, gate, offs, pos1,
         for c in range(CHUNKS):
             experts(c)
 
-        def product(c, t0, t1, r):
-            nc.vector.tensor_tensor(
-                prods[c][:, r, t0:t1], ys[c][:].indirect(pos_lists[r][:, t0 // 16 : t1 // 16]), gate_rows(c, r)[:, t0:t1], ALU.mult
-            )
+        def product(c, r):
+            nc.vector.tensor_tensor(prods[c][:, r, :], ys[c][:].indirect(pos_lists[r][:]), gates[c][:, r, :], ALU.mult)
 
         def store(c, t0, t1):
             nc.sync.dma_start(out=out[c * P : (c + 1) * P, t0:t1], in_=results[c][:, t0:t1])
 
         def sum_on_tensor(c):
             turned = late.tile([P, T], F32, name=f"turned{c}")
-            for t0, t1 in ((0, BANK), (BANK, T)):
+            spans = ((0, BANK), (BANK, T))
+            for t0, t1 in spans:
                 sums = psum.tile([P, t1 - t0], F32, name="sums", tag="bank")
                 for t in range(t0, t1, P):
                     for r in range(TOP):
@@ -218,31 +221,21 @@ def tile_moe_ecr_lin_silu_kernel(tc, xT, w_words, w_scales, b, gate, offs, pos1,
                             sums[:, t - t0 : t - t0 + P], prods[c][:, r, t : t + P], identity[:], start=(r == 0), stop=(r == TOP - 1), is_transpose=True
                         )
                 nc.scalar.copy(out=turned[:, t0:t1], in_=sums[:])
-            for t0, t1 in ((0, BANK), (BANK, T)):
+            for t0, t1 in spans:
                 back = psum.tile([P, t1 - t0], F32, name="back", tag="bank")
                 for t in range(t0, t1, P):
                     nc.tensor.transpose(back[:, t - t0 : t - t0 + P], turned[:, t : t + P], identity[:])
                 nc.scalar.copy(out=results[c][:, t0:t1], in_=back[:])
             store(c, 0, T)
 
-        def first_sum(c, t0, t1):
-            nc.vector.tensor_tensor(results[c][:, t0:t1], prods[c][:, 0, t0:t1], prods[c][:, 1, t0:t1], ALU.add)
-
-        def last_sum(c, t0, t1):
-            nc.vector.tensor_tensor(results[c][:, t0:t1], results[c][:, t0:t1], prods[c][:, 2, t0:t1], ALU.add)
-            store(c, t0, t1)
-
-        for c in range(CHUNKS - 1):
+        last = CHUNKS - 1
+        for c in range(CHUNKS):
             for r in range(TOP):
-                product(c, 0, T, r)
-            sum_on_tensor(c)
-        left, right = (CHUNKS - 1, 0, T // 2), (CHUNKS - 1, T // 2, T)
-        for r in range(TOP):
-            product(*left, r)
-        first_sum(*left)
-        product(*right, 0)
-        last_sum(*left)
-        product(*right, 1)
-        product(*right, 2)
-        first_sum(*right)
-        last_sum(*right)
+                product(c, r)
+            if c < last:
+                sum_on_tensor(c)
+        for t0, t1 in LAST_SPANS:
+            nc.vector.tensor_tensor(results[last][:, t0:t1], prods[last][:, 0, t0:t1], prods[last][:, 1, t0:t1], ALU.add)
+        for t0, t1 in LAST_SPANS:
+            nc.vector.tensor_tensor(results[last][:, t0:t1], results[last][:, t0:t1], prods[last][:, 2, t0:t1], ALU.add)
+            store(last, t0, t1)

from contextlib import ExitStack

import concourse.mybir as mybir
from concourse.masks import make_identity

K, T, E, C, N = 1536, 640, 8, 128, 384
TOP = 3
PAD = 64
SLOTS = E * C

FLOPS = 2 * K * N * SLOTS

F32 = mybir.dt.float32
BF16 = mybir.dt.bfloat16
I32 = mybir.dt.int32
U32 = mybir.dt.uint32
U16 = mybir.dt.uint16
U8 = mybir.dt.uint8
FP8X4 = mybir.dt.float8_e4m3fn_x4
FP4X4 = mybir.dt.float4_e2m1fn_x4
ACT = mybir.ActivationFunctionType
ALU = mybir.AluOpType

P = 128
PACK = 4
K_PASS = P * PACK
PASSES = K // K_PASS
CHUNKS = N // P
QUANT_PIECES = ((0, 256), (256, 512), (512, 640))
SHARED_COPY = ((0, 256, True), (256, 320, True), (320, 512, False), (512, 640, False))
SCALAR_COPY = ((0, 256, False), (256, 512, False), (512, 640, False))
COPY_PIECES = (SHARED_COPY, SCALAR_COPY, SHARED_COPY)
SLOT_PIECES = ((0, 384), (384, 768), (768, 1024))
DEFERRED = ((1, 0), (1, 1), (1, 2))
W_GROUP = 2 * PASSES
EARLY_W_GROUPS = 2
BANK = 512
LAST_SPANS = ((0, 384), (384, 640))
SHIFT_ROWS = ((0, 64), (64, 96), (96, 100))


def tile_moe_ecr_lin_silu_kernel(tc, xT, w_words, w_scales, b, gate, offs, pos1, pos2, pos3, out):
    nc = tc.nc
    with ExitStack() as ctx:
        keep = ctx.enter_context(tc.tile_pool(name="keep", bufs=1))
        psum = ctx.enter_context(tc.psum_pool(name="psum", bufs=8))

        slot_list = keep.tile([P, SLOTS // 16], U16, name="slot_list")
        pos_lists = [keep.tile([P, T // 16], U16, name=f"pos_list{r}") for r in range(TOP)]
        bias = keep.tile([P, CHUNKS, E], F32, name="bias")
        tok_codes = [keep.tile([P, T], U32, name=f"tok_codes{a}", align_bytes=64) for a in range(PASSES)]
        slot_codes = {
            (a, s): keep.tile([P, s1 - s0], U32, name=f"slot_codes{a}_{s0}", align_bytes=64)
            for a in range(PASSES)
            for s, (s0, s1) in enumerate(SLOT_PIECES)
            if (a, s) not in DEFERRED
        }
        slot_scales = [keep.tile([P, SLOTS], U8, name=f"slot_scales{a}", align_bytes=64) for a in range(PASSES)]
        w_codes01 = [keep.tile([P, W_GROUP, 4 * P], U8, name=f"w_codes01_{h}", align_bytes=64) for h in range(EARLY_W_GROUPS)]
        w_plane01 = keep.tile([P, E * PASSES, 2 * P], U8, name="w_plane01", align_bytes=64)
        identity = keep.tile([P, P], F32, name="identity")
        ys = [keep.tile([P, SLOTS + PAD], F32, name=f"y{c}") for c in range(CHUNKS)]
        zeros = keep.tile([P, PAD], F32, name="zeros")
        prods = [keep.tile([P, TOP, T], F32, name=f"prods{c}") for c in range(CHUNKS)]
        results = [keep.tile([P, T], F32, name=f"result{c}") for c in range(CHUNKS)]

        with tc.tile_pool(name="stage", bufs=1) as stage:
            raw = [stage.tile([P, PACK, T], F32, name=f"raw{a}") for a in range(PASSES)]
            grouped = [stage.tile([P, T, PACK], BF16, name=f"grouped{a}", align_bytes=64) for a in range(PASSES)]
            tok_scales = stage.tile([P, T], U8, name="tok_scales", align_bytes=64)

            nc.vector.memset(zeros[:], 0.0)
            nc.scalar.activation(out=ys[0][:, SLOTS:], in_=zeros[:], func=ACT.Silu)
            nc.vector.memset(tok_scales[:].bitcast(I32), 0)
            nc.vector.memset(w_plane01[:].rearrange("p g n -> p (g n)").bitcast(I32), 0)
            for a in range(1, PASSES):
                nc.vector.memset(slot_scales[a][:].bitcast(I32), 0)
            for c in range(1, CHUNKS):
                nc.vector.memset(ys[c][:, SLOTS:], 0.0)
            make_identity(nc, identity[:])

            def load_x(a):
                rows = xT[a * K_PASS : (a + 1) * K_PASS, :].rearrange("(p j) t -> p j t", j=PACK)
                nc.sync.dma_start(out=raw[a][:], in_=rows)

            def load_w(codes, g0, g1, n0, n1):
                words = w_words.rearrange("e a p b -> p (e a) b")
                nc.sync.dma_start(out=codes[:].bitcast(I32), in_=words[:, g0:g1, 2 * n0 : 2 * n1].bitcast(I32))

            def load_planes(plane, n0, n1):
                rows = w_scales.rearrange("e a q n -> q (e a) n")
                for quad in range(4):
                    nc.sync.dma_start(
                        out=plane[32 * quad : 32 * quad + 4, :, :].bitcast(I32),
                        in_=rows[4 * quad : 4 * quad + 4, :, n0:n1].bitcast(I32),
                    )

            def load_gates(c, r0, r1):
                nc.sync.dma_start(out=gates[c][:, r0:r1, :], in_=gate[r0:r1, c * P : (c + 1) * P, :].rearrange("r p t -> p r t"))

            load_x(0)
            nc.sync.dma_start(slot_list[:], offs)
            load_x(1)
            load_x(2)
            nc.sync.dma_start(out=bias[:], in_=b.rearrange("(c p) e -> p c e", p=P))
            for r, pos in enumerate((pos1, pos2, pos3)):
                nc.sync.dma_start(pos_lists[r][:], pos)
            load_planes(w_plane01, 0, 2 * P)
            for h in range(EARLY_W_GROUPS):
                load_w(w_codes01[h], h * W_GROUP, (h + 1) * W_GROUP, 0, 2 * P)

            def interleave(a, t0, t1, on_vector):
                src = raw[a][:, :, t0:t1].rearrange("p j (c i) -> p c j i", i=4)
                dst = grouped[a][:, t0:t1, :].rearrange("p (c i) j -> p c j i", i=4)
                if on_vector:
                    nc.vector.tensor_copy(out=dst, in_=src)
                else:
                    nc.scalar.activation(out=dst, in_=src, func=ACT.Copy)

            def quantize(a, t0, t1):
                nc.vector.quantize_mx(
                    out=tok_codes[a][:, t0:t1].bitcast(FP8X4),
                    scales=tok_scales[4 * a :, t0:t1],
                    in_=grouped[a][:, t0:t1, :].rearrange("p t j -> p (t j)"),
                )

            def gather_words(a, s):
                s0, s1 = SLOT_PIECES[s]
                nc.vector.tensor_copy(slot_codes[a, s][:], tok_codes[a][:].indirect(slot_list[:, s0 // 16 : s1 // 16]))

            def gather_bytes(s):
                s0, s1 = SLOT_PIECES[s]
                nc.vector.tensor_copy(slot_scales[0][:, s0:s1], tok_scales[:].indirect(slot_list[:, s0 // 16 : s1 // 16]))

            def shift(s0, s1):
                for a in range(1, PASSES):
                    for r0, r1 in SHIFT_ROWS:
                        nc.sync.dma_start(
                            out=slot_scales[a][r0:r1, s0:s1].bitcast(I32),
                            in_=slot_scales[0][r0 + 4 * a : r1 + 4 * a, s0:s1].bitcast(I32),
                        )

            for a in range(PASSES):
                for piece in COPY_PIECES[a]:
                    interleave(a, *piece)
                for piece in QUANT_PIECES:
                    quantize(a, *piece)
                if a < PASSES - 1:
                    for s in range(len(SLOT_PIECES)):
                        if (a, s) not in DEFERRED:
                            gather_words(a, s)
            for s in range(len(SLOT_PIECES)):
                gather_bytes(s)
            shift(0, SLOTS)

        late = ctx.enter_context(tc.tile_pool(name="late", bufs=1))
        for a, s in DEFERRED:
            s0, s1 = SLOT_PIECES[s]
            slot_codes[a, s] = late.tile([P, s1 - s0], U32, name=f"slot_codes{a}_{s0}", align_bytes=64)
        for s in range(len(SLOT_PIECES)):
            gather_words(PASSES - 1, s)
            if (1, s) in DEFERRED:
                gather_words(1, s)

        half = E * PASSES // 2
        for h in range(EARLY_W_GROUPS, E * PASSES // W_GROUP):
            w_codes01.append(late.tile([P, W_GROUP, 4 * P], U8, name=f"w_codes01_{h}", align_bytes=64))
            load_w(w_codes01[h], h * W_GROUP, (h + 1) * W_GROUP, 0, 2 * P)
        w_codes2 = [late.tile([P, half, 2 * P], U8, name=f"w_codes2_{h}", align_bytes=64) for h in range(2)]
        w_plane2 = late.tile([P, E * PASSES, P], U8, name="w_plane2", align_bytes=64)
        gates = [late.tile([P, TOP, T], F32, name=f"gates{c}") for c in range(CHUNKS)]
        nc.gpsimd.memset(w_plane2[:].rearrange("p g n -> p (g n)").bitcast(I32), 0)
        load_gates(0, 0, 1)
        load_gates(0, 1, TOP)
        load_planes(w_plane2, 2 * P, N)
        load_gates(1, 0, 1)
        load_w(w_codes2[0], 0, half, 2 * P, N)
        load_gates(1, 1, 2)
        load_w(w_codes2[1], half, 2 * half, 2 * P, N)
        load_gates(1, 2, 3)
        load_gates(2, 0, 1)
        load_gates(2, 1, TOP)

        def experts(c):
            for e in range(E):
                acc = psum.tile([P, C], F32, name="acc", tag="bank")
                cols = slice(e * C, (e + 1) * C)
                s = [s0 <= e * C < s1 for s0, s1 in SLOT_PIECES].index(True)
                in_piece = slice(e * C - SLOT_PIECES[s][0], (e + 1) * C - SLOT_PIECES[s][0])
                for a in range(PASSES):
                    g = e * PASSES + a
                    w_code = w_codes01[g // W_GROUP][:, g % W_GROUP, c * 2 * P : (c + 1) * 2 * P] if c < 2 else w_codes2[g // half][:, g % half, :]
                    nc.tensor.matmul_mx(
                        out=acc[:],
                        lhsT=w_code.bitcast(FP4X4),
                        lhsT_scale=w_plane01[:, g, c * P : (c + 1) * P] if c < 2 else w_plane2[:, g, :],
                        rhs=slot_codes[a, s][:, in_piece].bitcast(FP8X4),
                        rhs_scale=slot_scales[a][:, cols],
                        start=(a == 0),
                        stop=(a == PASSES - 1),
                    )
                nc.scalar.activation(out=ys[c][:, cols], in_=acc[:], func=ACT.Silu, bias=bias[:, c, e : e + 1])

        for c in range(CHUNKS):
            experts(c)

        def product(c, r):
            nc.vector.tensor_tensor(prods[c][:, r, :], ys[c][:].indirect(pos_lists[r][:]), gates[c][:, r, :], ALU.mult)

        def store(c, t0, t1):
            nc.sync.dma_start(out=out[c * P : (c + 1) * P, t0:t1], in_=results[c][:, t0:t1])

        def sum_on_tensor(c):
            turned = late.tile([P, T], F32, name=f"turned{c}")
            spans = ((0, BANK), (BANK, T))
            for t0, t1 in spans:
                sums = psum.tile([P, t1 - t0], F32, name="sums", tag="bank")
                for t in range(t0, t1, P):
                    for r in range(TOP):
                        nc.tensor.matmul(
                            sums[:, t - t0 : t - t0 + P], prods[c][:, r, t : t + P], identity[:], start=(r == 0), stop=(r == TOP - 1), is_transpose=True
                        )
                nc.scalar.copy(out=turned[:, t0:t1], in_=sums[:])
            for t0, t1 in spans:
                back = psum.tile([P, t1 - t0], F32, name="back", tag="bank")
                for t in range(t0, t1, P):
                    nc.tensor.transpose(back[:, t - t0 : t - t0 + P], turned[:, t : t + P], identity[:])
                nc.scalar.copy(out=results[c][:, t0:t1], in_=back[:])
            store(c, 0, T)

        last = CHUNKS - 1
        for c in range(CHUNKS):
            for r in range(TOP):
                product(c, r)
            if c < last:
                sum_on_tensor(c)
        for t0, t1 in LAST_SPANS:
            nc.vector.tensor_tensor(results[last][:, t0:t1], prods[last][:, 0, t0:t1], prods[last][:, 1, t0:t1], ALU.add)
        for t0, t1 in LAST_SPANS:
            nc.vector.tensor_tensor(results[last][:, t0:t1], results[last][:, t0:t1], prods[last][:, 2, t0:t1], ALU.add)
            store(last, t0, t1)
